import numpy as np, ml_dtypes
CORES = [49,52,55,57,60,63,65,68,71,73,76,79]
N = 12
KB, QP = 1, 128
WB = 2
def setup_inputs(rng):
    q = rng.standard_normal((N, 128, QP), dtype=np.float32) / 4; k = rng.standard_normal((N, 128, KB * 128), dtype=np.float32)
    a = 2 * np.pi * rng.random((N, QP)); s = 400 * rng.random((N, QP)) ** 1.5; q[:, 0, :] = s * np.cos(a); q[:, 1, :] = s * np.sin(a); q[:, 2, :] = 150 * rng.standard_normal((N, QP)); k[:, 2, :] = 1 + k[:, 2, :] / 50
    a = (2 * np.pi * rng.random() + np.pi / 2 * (rng.permutation(N).reshape(N, 1, 1) + 0.5) / N - 0.5 + (np.arange(KB).reshape(1, KB, 1) + rng.random((N, KB, 128))) / KB).reshape(N, KB * 128); k[:, 0, :] = np.cos(a); k[:, 1, :] = np.sin(a)
    return {"q": q.astype(ml_dtypes.bfloat16), "k": k.astype(ml_dtypes.bfloat16), "v": rng.standard_normal((N, 128, KB * 128), dtype=np.float32).astype(ml_dtypes.bfloat16)}
def setup_inputs_big(rng):
    d = setup_inputs(rng)
    for k in ("v",): d[k] = (d[k].astype(np.float32) * 1048576.0).astype(d[k].dtype)
    return d
def setup_inputs_small(rng):
    d = setup_inputs(rng)
    for k in ("v",): d[k] = (d[k].astype(np.float32) * (1 / 1048576.0)).astype(d[k].dtype)
    return d
def reference(q, k, v):
    Q, K, V = q.astype(np.float64), k.astype(np.float64), v.astype(np.float64)
    y = np.zeros((N, QP, 128))
    for r in range(N):
        js = list(range(max(0, r - WB), r + 1))
        S = np.concatenate([K[j].T @ Q[r] for j in js], axis=0)
        P = np.exp(S - S.max(axis=0)); P = P / P.sum(axis=0)
        y[r] = P.T @ np.concatenate([V[j][:, 128 * b:128 * b + 128] for j in js for b in range(KB)], axis=0)
    return {"y": y.astype(ml_dtypes.bfloat16)}

@@ -1,0 +1,188 @@
+from concourse.bass import DstId, RemoteDMATransfer
+from concourse.mybir import AluOpType, AxisListType, ActivationFunctionType
+
+WINDOW = 2
+SLOTS = WINDOW + 1
+F = 128
+SLOT = 2 * F
+ENGINES = 8
+NEV = 48
+
+SCRATCH = {
+    "kv": ("sbuf", [128, SLOTS * SLOT], "bfloat16"),
+    "qs": ("sbuf", [128, F], "bfloat16"),
+    "ones": ("sbuf", [128, F], "bfloat16"),
+    "ident": ("sbuf", [128, F], "bfloat16"),
+    "cols": ("sbuf", [128, 64], "float32"),
+    "ysb": ("sbuf", [128, F], "bfloat16"),
+    "po": ("psum", [128, 512], "float32"),
+}
+for _b in range(SLOTS):
+    SCRATCH["p%d" % _b] = ("sbuf", [128, F], "bfloat16")
+    SCRATCH["t%d" % _b] = ("sbuf", [128, F], "bfloat16")
+    SCRATCH["d%d" % _b] = ("sbuf", [128, F], "bfloat16")
+    SCRATCH["acc%d" % _b] = ("sbuf", [128, F], "bfloat16")
+    SCRATCH["ps%d" % _b] = ("psum", [128, 512], "float32")
+    SCRATCH["pt%d" % _b] = ("psum", [128, 1024], "bfloat16")
+
+SEMAPHORES = ["ld", "sent"] + ["arr%d" % _s for _s in range(SLOTS)] + ["e%d" % _i for _i in range(NEV)]
+
+
+def routes(cores, topo):
+    hops = []
+    for j in range(len(cores)):
+        dests = [t for t in range(j + 1, j + 1 + WINDOW) if t < len(cores)]
+        near = [t for t in dests if topo.chip(cores[t]) == topo.chip(cores[j])]
+        landed = []
+        for t in near:
+            hops.append((j, j, t))
+        for t in dests:
+            if t in near:
+                continue
+            inside = [u for u in landed if topo.chip(cores[u]) == topo.chip(cores[t])]
+            if inside:
+                hops.append((inside[0], j, t))
+            else:
+                gate = [h for h in [j] + near if topo.may_write(cores[h], cores[t])][0]
+                hops.append((gate, j, t))
+            landed.append(t)
+    return hops
+
+
+def pick(mask, n):
+    bits = [b for b in range(mask.bit_length()) if (mask >> b) & 1]
+    n = min(n, len(bits))
+    out = 0
+    for b in bits[::len(bits) // n][:n]:
+        out |= 1 << b
+    return out
+
+
+def rank_program(g, core, T, topo):
+    rank = T.rank_of(core)
+    if rank is None:
+        return
+    cores = T.cores
+    Exp, Copy = ActivationFunctionType.Exp, ActivationFunctionType.Copy
+    mult, add = AluOpType.mult, AluOpType.add
+
+    queues = {"pe": g.tensor, "ve": g.vector, "ac": g.scalar, "sp": g.sync, "gp": g}
+    waited = {name: [] for name in queues}
+    used = [0]
+
+    def after(qn, events):
+        for ev in events:
+            if ev not in waited[qn]:
+                queues[qn].wait_ge(T.sem[ev[0]], ev[1])
+                waited[qn].append(ev)
+
+    def done(instr, n=1):
+        name = "e%d" % used[0]
+        used[0] += 1
+        instr.then_inc(T.sem[name], n)
+        return (name, n)
+
+    def K(j):
+        return T.kv[:, (j % SLOTS) * SLOT:(j % SLOTS) * SLOT + F]
+
+    def V(j):
+        return T.kv[:, (j % SLOTS) * SLOT + F:(j % SLOTS + 1) * SLOT]
+
+    def KV(j):
+        return T.kv[:, (j % SLOTS) * SLOT:(j % SLOTS + 1) * SLOT]
+
+    def col(i):
+        return T.cols[:, 4 * i:4 * i + 1]
+
+    def engines(src, dst):
+        return pick(topo.mask(cores[src], cores[dst]), ENGINES)
+
+    def width(m):
+        return bin(m).count("1")
+
+    g.sync.dma_start(K(rank), T.k[:, :]).then_inc(T.sem.ld, 16)
+    g.scalar.dma_start(V(rank), T.v[:, :]).then_inc(T.sem.ld, 16)
+    q_in = done(g.sync.dma_start(T.qs[:, :], T.q[:, :]), 16)
+    here = {rank: ("ld", 32)}
+
+    ones = done(g.vector.memset(T.ones[:, :], 1.0))
+    after("gp", [ones])
+    ident = done(g.affine_select(T.ident[:, :], T.ones[:, :], [[-1, F]], AluOpType.is_equal, 0.0, 0, 1))
+
+    hops = routes(cores, topo)
+    for (h, j, t) in hops:
+        if t == rank:
+            here[j] = ("arr%d" % (j % SLOTS), width(engines(h, t)))
+    sent = 0
+    groups = []
+    for (h, j, t) in sorted([x for x in hops if x[0] == rank], key=lambda x: (-x[1], x[2])):
+        m = engines(h, t)
+        if groups and groups[-1][0] == j and groups[-1][1] == m:
+            groups[-1][2].append(t)
+        else:
+            groups.append((j, m, [t]))
+    for (j, m, ts) in groups:
+        after("gp", [here[j]])
+        arr = T.sem["arr%d" % (j % SLOTS)]
+        if len(ts) == 1:
+            rid, pid, _ = topo.addr(cores[ts[0]])
+            g.remote_dma(KV(j), KV(j), arr, T.sem.sent, pid, rid, m)
+        else:
+            ids = [DstId(rid=topo.addr(cores[t])[0], pnc=topo.addr(cores[t])[1]) for t in ts]
+            g.remote_dma_fused([RemoteDMATransfer(dst_ids=ids, dma_engine_mask=m, remote_sem=arr,
+                                                  srcs=[KV(j)], dsts=[KV(j) for _ in ts])], local_sem=T.sem.sent)
+        sent += width(m)
+    if sent:
+        after("gp", [("sent", sent)])
+
+    blocks = [rank - d for d in range(SLOTS) if rank - d >= 0]
+    m_col = acc_ev = l_ev = None
+    l_col = None
+    for b, j in enumerate(blocks):
+        last = b == len(blocks) - 1
+        ps, pt = T["ps%d" % b], T["pt%d" % b]
+        p, t, d = T["p%d" % b], T["t%d" % b], T["d%d" % b]
+        neg_m, l_j, w, l_new = col(b), col(4 + b), col(8 + b), col(12 + b)
+
+        after("pe", [q_in, here[j]] + ([m_col] if b else []))
+        s_ev = done(g.tensor.matmul(ps[:, 0:F], T.qs[:, :], K(j), True, True))
+        after("ve", [s_ev])
+        max_ev = done(g.vector.tensor_reduce(neg_m, ps[:, 0:F + (1 if b else 0)], AxisListType.X, AluOpType.max,
+                                             negate=True))
+        after("ac", [max_ev])
+        if b:
+            w_ev = done(g.scalar.activation(w, col(b - 1), Exp, bias=neg_m, scale=-1.0))
+        p_ev = done(g.scalar.activation(p[:, :], ps[:, 0:F], Exp, bias=neg_m, scale=1.0, accum_out=l_j))
+        if b:
+            after("ve", [w_ev, ident])
+            d_ev = done(g.vector.tensor_scalar(d[:, :], T.ident[:, :], w, None, mult))
+        if not last:
+            after("ve", [max_ev])
+            m_col = done(g.vector.tensor_scalar(T["ps%d" % (b + 1)][:, F:F + 1], neg_m, -1.0, None, mult))
+
+        after("pe", [p_ev, ident])
+        t_ev = done(g.tensor.transpose(pt[:, 0:F], p[:, :], T.ident[:, :]))
+        after("ac", [t_ev])
+        c_ev = done(g.scalar.activation(t[:, :], pt[:, 0:F], Copy))
+        if b:
+            after("pe", [d_ev, acc_ev])
+            g.tensor.matmul(T.po[:, 0:F], d[:, :], T["acc%d" % (b - 1)][:, :], True, False)
+        after("pe", [c_ev])
+        o_ev = done(g.tensor.matmul(T.po[:, 0:F], t[:, :], V(j), not b, True))
+
+        if b:
+            after("ve", [p_ev, l_ev])
+            l_ev = done(g.vector.tensor_scalar(l_new, w, l_col, l_j, mult, add))
+            l_col = l_new
+        else:
+            l_ev, l_col = p_ev, l_j
+        if last:
+            after("ve", [l_ev])
+            r_ev = done(g.vector.reciprocal(col(3), l_col))
+            after("ve", [o_ev, r_ev])
+            y_ev = done(g.vector.tensor_scalar(T.ysb[:, :], T.po[:, 0:F], col(3), None, mult))
+            after("sp", [y_ev])
+            after("sp", [done(g.sync.dma_start(T.y[:, :], T.ysb[:, :]), 16)])
+        else:
+            after("ve", [o_ev])
+            acc_ev = done(g.vector.tensor_copy(T["acc%d" % b][:, :], T.po[:, 0:F]))

@@ -5,11 +5,14 @@ WINDOW = 2
 SLOTS = WINDOW + 1
 F = 128
 SLOT = 2 * F
-ENGINES = 8
+ROW_ENGINES = 8
+RUN_ENGINES = 4
 NEV = 48
 
 SCRATCH = {
     "kv": ("sbuf", [128, SLOTS * SLOT], "bfloat16"),
+    "kd": ("dram", [SLOTS, 128, F], "bfloat16"),
+    "vd": ("dram", [SLOTS, 128, F], "bfloat16"),
     "qs": ("sbuf", [128, F], "bfloat16"),
     "ones": ("sbuf", [128, F], "bfloat16"),
     "ident": ("sbuf", [128, F], "bfloat16"),
@@ -25,27 +28,32 @@ for _b in range(SLOTS):
     SCRATCH["ps%d" % _b] = ("psum", [128, 512], "float32")
     SCRATCH["pt%d" % _b] = ("psum", [128, 1024], "bfloat16")
 
-SEMAPHORES = ["ld", "sent"] + ["arr%d" % _s for _s in range(SLOTS)] + ["e%d" % _i for _i in range(NEV)]
+SEMAPHORES = (["ld", "st", "sent"] + ["%s%d" % (_n, _s) for _n in ("arr", "dar", "ak", "av") for _s in range(SLOTS)]
+              + ["e%d" % _i for _i in range(NEV)])
 
 
-def routes(cores, topo):
+def plan(cores, topo):
     hops = []
     for j in range(len(cores)):
         dests = [t for t in range(j + 1, j + 1 + WINDOW) if t < len(cores)]
         near = [t for t in dests if topo.chip(cores[t]) == topo.chip(cores[j])]
-        landed = []
-        for t in near:
-            hops.append((j, j, t))
+        gates = []
+        chips = []
         for t in dests:
-            if t in near:
-                continue
-            inside = [u for u in landed if topo.chip(cores[u]) == topo.chip(cores[t])]
-            if inside:
-                hops.append((inside[0], j, t))
-            else:
-                gate = [h for h in [j] + near if topo.may_write(cores[h], cores[t])][0]
-                hops.append((gate, j, t))
-            landed.append(t)
+            if t not in near and topo.chip(cores[t]) not in chips:
+                chips.append(topo.chip(cores[t]))
+        for c in chips:
+            far = [t for t in dests if topo.chip(cores[t]) == c]
+            gate = [h for h in [j] + near if topo.may_write(cores[h], cores[far[0]])][0]
+            if gate != j and gate not in gates:
+                gates.append(gate)
+            hops.append((gate, j, far[0], "split"))
+            for t in far[1:]:
+                hops.append((gate, j, t, "row" if gate == j else "split"))
+        for t in near:
+            if t in gates:
+                hops.append((j, j, t, "run"))
+            hops.append((j, j, t, "row"))
     return hops
 
 
@@ -94,95 +102,146 @@ def rank_program(g, core, T, topo):
     def col(i):
         return T.cols[:, 4 * i:4 * i + 1]
 
-    def engines(src, dst):
-        return pick(topo.mask(cores[src], cores[dst]), ENGINES)
-
     def width(m):
         return bin(m).count("1")
 
+    def halves(m):
+        bits = [b for b in range(m.bit_length()) if (m >> b) & 1]
+        return sum(1 << b for b in bits[0::2]), sum(1 << b for b in bits[1::2])
+
+    def engines(h, t, form):
+        return pick(topo.mask(cores[h], cores[t]), RUN_ENGINES if form == "run" else ROW_ENGINES)
+
+    hops = plan(cores, topo)
+    mine = [x for x in hops if x[0] == rank]
+    staged = any(j == rank and form != "row" for (h, j, t, form) in mine)
+
+    if staged:
+        g.sync.dma_start(T.kd[rank % SLOTS], T.k[:, :]).then_inc(T.sem.st, 16)
+        g.scalar.dma_start(T.vd[rank % SLOTS], T.v[:, :]).then_inc(T.sem.st, 16)
     g.sync.dma_start(K(rank), T.k[:, :]).then_inc(T.sem.ld, 16)
     g.scalar.dma_start(V(rank), T.v[:, :]).then_inc(T.sem.ld, 16)
     q_in = done(g.sync.dma_start(T.qs[:, :], T.q[:, :]), 16)
-    here = {rank: ("ld", 32)}
+    k_here, v_here = {rank: ("ld", 32)}, {rank: ("ld", 32)}
+    indram = {rank: ("st", 32)} if staged else {}
 
     ones = done(g.vector.memset(T.ones[:, :], 1.0))
     after("gp", [ones])
     ident = done(g.affine_select(T.ident[:, :], T.ones[:, :], [[-1, F]], AluOpType.is_equal, 0.0, 0, 1))
 
-    hops = routes(cores, topo)
-    for (h, j, t) in hops:
+    for (h, j, t, form) in hops:
         if t == rank:
-            here[j] = ("arr%d" % (j % SLOTS), width(engines(h, t)))
+            n, s = width(engines(h, t, form)), j % SLOTS
+            if form == "run":
+                indram[j] = ("dar%d" % s, n)
+            elif form == "row":
+                k_here[j] = v_here[j] = ("arr%d" % s, n)
+            else:
+                k_here[j], v_here[j] = ("ak%d" % s, n), ("av%d" % s, n)
+
+    calls = []
+    for (h, j, t, form) in mine:
+        m, own = engines(h, t, form), j == rank
+        if form == "run":
+            calls.append([0, j, "run", m, [t]])
+        elif form == "row":
+            same = [c for c in calls if c[1:4] == [j, "row", m]]
+            if same:
+                same[0][4].append(t)
+            else:
+                calls.append([2, j, "row", m, [t]])
+        else:
+            calls.append([1 if own else 3, j, "k", m, [t]])
+            calls.append([4 if own else 5, j, "v", m, [t]])
     sent = 0
-    groups = []
-    for (h, j, t) in sorted([x for x in hops if x[0] == rank], key=lambda x: (-x[1], x[2])):
-        m = engines(h, t)
-        if groups and groups[-1][0] == j and groups[-1][1] == m:
-            groups[-1][2].append(t)
-        else:
-            groups.append((j, m, [t]))
-    for (j, m, ts) in groups:
-        after("gp", [here[j]])
-        arr = T.sem["arr%d" % (j % SLOTS)]
-        if len(ts) == 1:
-            rid, pid, _ = topo.addr(cores[ts[0]])
-            g.remote_dma(KV(j), KV(j), arr, T.sem.sent, pid, rid, m)
-        else:
-            ids = [DstId(rid=topo.addr(cores[t])[0], pnc=topo.addr(cores[t])[1]) for t in ts]
-            g.remote_dma_fused([RemoteDMATransfer(dst_ids=ids, dma_engine_mask=m, remote_sem=arr,
+    for (_, j, piece, m, ts) in sorted(calls, key=lambda c: (c[0], -c[1], c[4][0])):
+        s = j % SLOTS
+        ids = [DstId(rid=topo.addr(cores[t])[0], pnc=topo.addr(cores[t])[1]) for t in sorted(ts)]
+        if piece == "run":
+            after("gp", [indram[j]])
+            mk, mv = halves(m)
+            g.remote_dma_fused([RemoteDMATransfer(dst_ids=ids, dma_engine_mask=mk, remote_sem=T.sem["dar%d" % s],
+                                                  srcs=[T.kd[s]], dsts=[T.kd[s]]),
+                                RemoteDMATransfer(dst_ids=ids, dma_engine_mask=mv, remote_sem=T.sem["dar%d" % s],
+                                                  srcs=[T.vd[s]], dsts=[T.vd[s]])], local_sem=T.sem.sent)
+        elif piece == "row":
+            after("gp", [k_here[j], v_here[j]])
+            g.remote_dma_fused([RemoteDMATransfer(dst_ids=ids, dma_engine_mask=m, remote_sem=T.sem["arr%d" % s],
                                                   srcs=[KV(j)], dsts=[KV(j) for _ in ts])], local_sem=T.sem.sent)
+        else:
+            dst, dram, ev, name = (K(j), T.kd[s], k_here, "ak%d") if piece == "k" else (V(j), T.vd[s], v_here, "av%d")
+            after("gp", [indram[j] if j in indram else ev[j]])
+            g.remote_dma(dst, dram if j in indram else dst, T.sem[name % s], T.sem.sent, ids[0].pnc, ids[0].rid, m)
         sent += width(m)
     if sent:
         after("gp", [("sent", sent)])
 
     blocks = [rank - d for d in range(SLOTS) if rank - d >= 0]
-    m_col = acc_ev = l_ev = None
-    l_col = None
-    for b, j in enumerate(blocks):
-        last = b == len(blocks) - 1
-        ps, pt = T["ps%d" % b], T["pt%d" % b]
-        p, t, d = T["p%d" % b], T["t%d" % b], T["d%d" % b]
-        neg_m, l_j, w, l_new = col(b), col(4 + b), col(8 + b), col(12 + b)
+    nb = len(blocks)
+    ev = {}
+    l_cols = {}
 
-        after("pe", [q_in, here[j]] + ([m_col] if b else []))
+    def neg_m(b):
+        return col(b)
+
+    def w_col(b):
+        return col(8 + b)
+
+    def step_s(b):
+        j, ps = blocks[b], T["ps%d" % b]
+        after("pe", [q_in, k_here[j]] + ([ev["m", b - 1]] if b else []))
         s_ev = done(g.tensor.matmul(ps[:, 0:F], T.qs[:, :], K(j), True, True))
         after("ve", [s_ev])
-        max_ev = done(g.vector.tensor_reduce(neg_m, ps[:, 0:F + (1 if b else 0)], AxisListType.X, AluOpType.max,
+        max_ev = done(g.vector.tensor_reduce(neg_m(b), ps[:, 0:F + (1 if b else 0)], AxisListType.X, AluOpType.max,
                                              negate=True))
         after("ac", [max_ev])
+        ev["p", b] = done(g.scalar.activation(T["p%d" % b][:, :], ps[:, 0:F], Exp, bias=neg_m(b), scale=1.0,
+                                              accum_out=col(4 + b)))
         if b:
-            w_ev = done(g.scalar.activation(w, col(b - 1), Exp, bias=neg_m, scale=-1.0))
-        p_ev = done(g.scalar.activation(p[:, :], ps[:, 0:F], Exp, bias=neg_m, scale=1.0, accum_out=l_j))
-        if b:
-            after("ve", [w_ev, ident])
-            d_ev = done(g.vector.tensor_scalar(d[:, :], T.ident[:, :], w, None, mult))
-        if not last:
+            ev["w", b] = done(g.scalar.activation(w_col(b), neg_m(b - 1), Exp, bias=neg_m(b), scale=-1.0))
+        if b < nb - 1:
             after("ve", [max_ev])
-            m_col = done(g.vector.tensor_scalar(T["ps%d" % (b + 1)][:, F:F + 1], neg_m, -1.0, None, mult))
+            ev["m", b] = done(g.vector.tensor_scalar(T["ps%d" % (b + 1)][:, F:F + 1], neg_m(b), -1.0, None, mult))
 
-        after("pe", [p_ev, ident])
-        t_ev = done(g.tensor.transpose(pt[:, 0:F], p[:, :], T.ident[:, :]))
+    def step_t(b):
+        pt = T["pt%d" % b]
+        after("pe", [ev["p", b], ident])
+        t_ev = done(g.tensor.transpose(pt[:, 0:F], T["p%d" % b][:, :], T.ident[:, :]))
         after("ac", [t_ev])
-        c_ev = done(g.scalar.activation(t[:, :], pt[:, 0:F], Copy))
+        ev["c", b] = done(g.scalar.activation(T["t%d" % b][:, :], pt[:, 0:F], Copy))
         if b:
-            after("pe", [d_ev, acc_ev])
-            g.tensor.matmul(T.po[:, 0:F], d[:, :], T["acc%d" % (b - 1)][:, :], True, False)
-        after("pe", [c_ev])
-        o_ev = done(g.tensor.matmul(T.po[:, 0:F], t[:, :], V(j), not b, True))
+            after("ve", [ev["w", b], ident])
+            ev["d", b] = done(g.vector.tensor_scalar(T["d%d" % b][:, :], T.ident[:, :], w_col(b), None, mult))
 
+    def step_o(b):
+        j = blocks[b]
         if b:
-            after("ve", [p_ev, l_ev])
-            l_ev = done(g.vector.tensor_scalar(l_new, w, l_col, l_j, mult, add))
-            l_col = l_new
+            after("pe", [ev["d", b], ev["acc", b - 1]])
+            g.tensor.matmul(T.po[:, 0:F], T["d%d" % b][:, :], T["acc%d" % (b - 1)][:, :], True, False)
+        after("pe", [ev["c", b], v_here[j]])
+        o_ev = done(g.tensor.matmul(T.po[:, 0:F], T["t%d" % b][:, :], V(j), not b, True))
+        if b:
+            after("ve", [ev["p", b], ev["w", b], ev["l", b - 1]])
+            ev["l", b] = done(g.vector.tensor_scalar(col(12 + b), w_col(b), l_cols[b - 1], col(4 + b), mult, add))
+            l_cols[b] = col(12 + b)
         else:
-            l_ev, l_col = p_ev, l_j
-        if last:
-            after("ve", [l_ev])
-            r_ev = done(g.vector.reciprocal(col(3), l_col))
+            ev["l", b], l_cols[b] = ev["p", b], col(4 + b)
+        if b == nb - 1:
+            after("ve", [ev["l", b]])
+            r_ev = done(g.vector.reciprocal(col(3), l_cols[b]))
             after("ve", [o_ev, r_ev])
             y_ev = done(g.vector.tensor_scalar(T.ysb[:, :], T.po[:, 0:F], col(3), None, mult))
             after("sp", [y_ev])
             after("sp", [done(g.sync.dma_start(T.y[:, :], T.ysb[:, :]), 16)])
         else:
             after("ve", [o_ev])
-            acc_ev = done(g.vector.tensor_copy(T["acc%d" % b][:, :], T.po[:, 0:F]))
+            ev["acc", b] = done(g.vector.tensor_copy(T["acc%d" % b][:, :], T.po[:, 0:F]))
+
+    order = []
+    for b in range(nb):
+        order += [(step_s, b), (step_t, b), (step_o, b)]
+    if nb > 2:
+        i = order.index((step_s, nb - 1))
+        order[i - 1], order[i] = order[i], order[i - 1]
+    for (step, b) in order:
+        step(b)

from concourse.bass import DstId, RemoteDMATransfer
from concourse.mybir import AluOpType, AxisListType, ActivationFunctionType

WINDOW = 2
SLOTS = WINDOW + 1
F = 128
SLOT = 2 * F
ROW_ENGINES = 8
RUN_ENGINES = 4
NEV = 48

SCRATCH = {
    "kv": ("sbuf", [128, SLOTS * SLOT], "bfloat16"),
    "kd": ("dram", [SLOTS, 128, F], "bfloat16"),
    "vd": ("dram", [SLOTS, 128, F], "bfloat16"),
    "qs": ("sbuf", [128, F], "bfloat16"),
    "ones": ("sbuf", [128, F], "bfloat16"),
    "ident": ("sbuf", [128, F], "bfloat16"),
    "cols": ("sbuf", [128, 64], "float32"),
    "ysb": ("sbuf", [128, F], "bfloat16"),
    "po": ("psum", [128, 512], "float32"),
}
for _b in range(SLOTS):
    SCRATCH["p%d" % _b] = ("sbuf", [128, F], "bfloat16")
    SCRATCH["t%d" % _b] = ("sbuf", [128, F], "bfloat16")
    SCRATCH["d%d" % _b] = ("sbuf", [128, F], "bfloat16")
    SCRATCH["acc%d" % _b] = ("sbuf", [128, F], "bfloat16")
    SCRATCH["ps%d" % _b] = ("psum", [128, 512], "float32")
    SCRATCH["pt%d" % _b] = ("psum", [128, 1024], "bfloat16")

SEMAPHORES = (["ld", "st", "sent"] + ["%s%d" % (_n, _s) for _n in ("arr", "dar", "ak", "av") for _s in range(SLOTS)]
              + ["e%d" % _i for _i in range(NEV)])


def plan(cores, topo):
    hops = []
    for j in range(len(cores)):
        dests = [t for t in range(j + 1, j + 1 + WINDOW) if t < len(cores)]
        near = [t for t in dests if topo.chip(cores[t]) == topo.chip(cores[j])]
        gates = []
        chips = []
        for t in dests:
            if t not in near and topo.chip(cores[t]) not in chips:
                chips.append(topo.chip(cores[t]))
        for c in chips:
            far = [t for t in dests if topo.chip(cores[t]) == c]
            gate = [h for h in [j] + near if topo.may_write(cores[h], cores[far[0]])][0]
            if gate != j and gate not in gates:
                gates.append(gate)
            hops.append((gate, j, far[0], "split"))
            for t in far[1:]:
                hops.append((gate, j, t, "row" if gate == j else "split"))
        for t in near:
            if t in gates:
                hops.append((j, j, t, "run"))
            hops.append((j, j, t, "row"))
    return hops


def pick(mask, n):
    bits = [b for b in range(mask.bit_length()) if (mask >> b) & 1]
    n = min(n, len(bits))
    out = 0
    for b in bits[::len(bits) // n][:n]:
        out |= 1 << b
    return out


def rank_program(g, core, T, topo):
    rank = T.rank_of(core)
    if rank is None:
        return
    cores = T.cores
    Exp, Copy = ActivationFunctionType.Exp, ActivationFunctionType.Copy
    mult, add = AluOpType.mult, AluOpType.add

    queues = {"pe": g.tensor, "ve": g.vector, "ac": g.scalar, "sp": g.sync, "gp": g}
    waited = {name: [] for name in queues}
    used = [0]

    def after(qn, events):
        for ev in events:
            if ev not in waited[qn]:
                queues[qn].wait_ge(T.sem[ev[0]], ev[1])
                waited[qn].append(ev)

    def done(instr, n=1):
        name = "e%d" % used[0]
        used[0] += 1
        instr.then_inc(T.sem[name], n)
        return (name, n)

    def K(j):
        return T.kv[:, (j % SLOTS) * SLOT:(j % SLOTS) * SLOT + F]

    def V(j):
        return T.kv[:, (j % SLOTS) * SLOT + F:(j % SLOTS + 1) * SLOT]

    def KV(j):
        return T.kv[:, (j % SLOTS) * SLOT:(j % SLOTS + 1) * SLOT]

    def col(i):
        return T.cols[:, 4 * i:4 * i + 1]

    def width(m):
        return bin(m).count("1")

    def halves(m):
        bits = [b for b in range(m.bit_length()) if (m >> b) & 1]
        return sum(1 << b for b in bits[0::2]), sum(1 << b for b in bits[1::2])

    def engines(h, t, form):
        return pick(topo.mask(cores[h], cores[t]), RUN_ENGINES if form == "run" else ROW_ENGINES)

    hops = plan(cores, topo)
    mine = [x for x in hops if x[0] == rank]
    staged = any(j == rank and form != "row" for (h, j, t, form) in mine)

    if staged:
        g.sync.dma_start(T.kd[rank % SLOTS], T.k[:, :]).then_inc(T.sem.st, 16)
        g.scalar.dma_start(T.vd[rank % SLOTS], T.v[:, :]).then_inc(T.sem.st, 16)
    g.sync.dma_start(K(rank), T.k[:, :]).then_inc(T.sem.ld, 16)
    g.scalar.dma_start(V(rank), T.v[:, :]).then_inc(T.sem.ld, 16)
    q_in = done(g.sync.dma_start(T.qs[:, :], T.q[:, :]), 16)
    k_here, v_here = {rank: ("ld", 32)}, {rank: ("ld", 32)}
    indram = {rank: ("st", 32)} if staged else {}

    ones = done(g.vector.memset(T.ones[:, :], 1.0))
    after("gp", [ones])
    ident = done(g.affine_select(T.ident[:, :], T.ones[:, :], [[-1, F]], AluOpType.is_equal, 0.0, 0, 1))

    for (h, j, t, form) in hops:
        if t == rank:
            n, s = width(engines(h, t, form)), j % SLOTS
            if form == "run":
                indram[j] = ("dar%d" % s, n)
            elif form == "row":
                k_here[j] = v_here[j] = ("arr%d" % s, n)
            else:
                k_here[j], v_here[j] = ("ak%d" % s, n), ("av%d" % s, n)

    calls = []
    for (h, j, t, form) in mine:
        m, own = engines(h, t, form), j == rank
        if form == "run":
            calls.append([0, j, "run", m, [t]])
        elif form == "row":
            same = [c for c in calls if c[1:4] == [j, "row", m]]
            if same:
                same[0][4].append(t)
            else:
                calls.append([2, j, "row", m, [t]])
        else:
            calls.append([1 if own else 3, j, "k", m, [t]])
            calls.append([4 if own else 5, j, "v", m, [t]])
    sent = 0
    for (_, j, piece, m, ts) in sorted(calls, key=lambda c: (c[0], -c[1], c[4][0])):
        s = j % SLOTS
        ids = [DstId(rid=topo.addr(cores[t])[0], pnc=topo.addr(cores[t])[1]) for t in sorted(ts)]
        if piece == "run":
            after("gp", [indram[j]])
            mk, mv = halves(m)
            g.remote_dma_fused([RemoteDMATransfer(dst_ids=ids, dma_engine_mask=mk, remote_sem=T.sem["dar%d" % s],
                                                  srcs=[T.kd[s]], dsts=[T.kd[s]]),
                                RemoteDMATransfer(dst_ids=ids, dma_engine_mask=mv, remote_sem=T.sem["dar%d" % s],
                                                  srcs=[T.vd[s]], dsts=[T.vd[s]])], local_sem=T.sem.sent)
        elif piece == "row":
            after("gp", [k_here[j], v_here[j]])
            g.remote_dma_fused([RemoteDMATransfer(dst_ids=ids, dma_engine_mask=m, remote_sem=T.sem["arr%d" % s],
                                                  srcs=[KV(j)], dsts=[KV(j) for _ in ts])], local_sem=T.sem.sent)
        else:
            dst, dram, ev, name = (K(j), T.kd[s], k_here, "ak%d") if piece == "k" else (V(j), T.vd[s], v_here, "av%d")
            after("gp", [indram[j] if j in indram else ev[j]])
            g.remote_dma(dst, dram if j in indram else dst, T.sem[name % s], T.sem.sent, ids[0].pnc, ids[0].rid, m)
        sent += width(m)
    if sent:
        after("gp", [("sent", sent)])

    blocks = [rank - d for d in range(SLOTS) if rank - d >= 0]
    nb = len(blocks)
    ev = {}
    l_cols = {}

    def neg_m(b):
        return col(b)

    def w_col(b):
        return col(8 + b)

    def step_s(b):
        j, ps = blocks[b], T["ps%d" % b]
        after("pe", [q_in, k_here[j]] + ([ev["m", b - 1]] if b else []))
        s_ev = done(g.tensor.matmul(ps[:, 0:F], T.qs[:, :], K(j), True, True))
        after("ve", [s_ev])
        max_ev = done(g.vector.tensor_reduce(neg_m(b), ps[:, 0:F + (1 if b else 0)], AxisListType.X, AluOpType.max,
                                             negate=True))
        after("ac", [max_ev])
        ev["p", b] = done(g.scalar.activation(T["p%d" % b][:, :], ps[:, 0:F], Exp, bias=neg_m(b), scale=1.0,
                                              accum_out=col(4 + b)))
        if b:
            ev["w", b] = done(g.scalar.activation(w_col(b), neg_m(b - 1), Exp, bias=neg_m(b), scale=-1.0))
        if b < nb - 1:
            after("ve", [max_ev])
            ev["m", b] = done(g.vector.tensor_scalar(T["ps%d" % (b + 1)][:, F:F + 1], neg_m(b), -1.0, None, mult))

    def step_t(b):
        pt = T["pt%d" % b]
        after("pe", [ev["p", b], ident])
        t_ev = done(g.tensor.transpose(pt[:, 0:F], T["p%d" % b][:, :], T.ident[:, :]))
        after("ac", [t_ev])
        ev["c", b] = done(g.scalar.activation(T["t%d" % b][:, :], pt[:, 0:F], Copy))
        if b:
            after("ve", [ev["w", b], ident])
            ev["d", b] = done(g.vector.tensor_scalar(T["d%d" % b][:, :], T.ident[:, :], w_col(b), None, mult))

    def step_o(b):
        j = blocks[b]
        if b:
            after("pe", [ev["d", b], ev["acc", b - 1]])
            g.tensor.matmul(T.po[:, 0:F], T["d%d" % b][:, :], T["acc%d" % (b - 1)][:, :], True, False)
        after("pe", [ev["c", b], v_here[j]])
        o_ev = done(g.tensor.matmul(T.po[:, 0:F], T["t%d" % b][:, :], V(j), not b, True))
        if b:
            after("ve", [ev["p", b], ev["w", b], ev["l", b - 1]])
            ev["l", b] = done(g.vector.tensor_scalar(col(12 + b), w_col(b), l_cols[b - 1], col(4 + b), mult, add))
            l_cols[b] = col(12 + b)
        else:
            ev["l", b], l_cols[b] = ev["p", b], col(4 + b)
        if b == nb - 1:
            after("ve", [ev["l", b]])
            r_ev = done(g.vector.reciprocal(col(3), l_cols[b]))
            after("ve", [o_ev, r_ev])
            y_ev = done(g.vector.tensor_scalar(T.ysb[:, :], T.po[:, 0:F], col(3), None, mult))
            after("sp", [y_ev])
            after("sp", [done(g.sync.dma_start(T.y[:, :], T.ysb[:, :]), 16)])
        else:
            after("ve", [o_ev])
            ev["acc", b] = done(g.vector.tensor_copy(T["acc%d" % b][:, :], T.po[:, 0:F]))

    order = []
    for b in range(nb):
        order += [(step_s, b), (step_t, b), (step_o, b)]
    if nb > 2:
        i = order.index((step_s, nb - 1))
        order[i - 1], order[i] = order[i], order[i - 1]
    for (step, b) in order:
        step(b)
